import numpy as np
import ml_dtypes


def mxq(x, axis, fmt="e4m3"):
    dtype, down = {"e4m3": (ml_dtypes.float8_e4m3fn, 7), "e5m2": (ml_dtypes.float8_e5m2, 14)}[fmt]
    v = np.moveaxis(np.asarray(x, np.float32).astype(ml_dtypes.bfloat16).astype(np.float64), axis, -1)
    blocks = v.reshape(v.shape[:-1] + (-1, 32))
    amax = np.abs(blocks).max(-1, keepdims=True)
    byte = np.maximum(np.where(amax > 0, np.frexp(amax)[1] - 1 + 127, 0) - down, 1)
    scale = np.exp2(byte - 127.0)
    codes = (blocks / scale).astype(np.float32).astype(dtype).astype(np.float64)
    return np.moveaxis((codes * scale).reshape(v.shape), -1, axis)


WIDE = False


def mx_kscale(k):
    if not WIDE:
        return np.ones(k)
    levels = np.array([10, -10, 5, -5, 0])
    if k % 512:
        return np.exp2(np.random.permutation(np.resize(levels, k // 32))).repeat(32)
    a = np.empty((k // 512, 16))
    for p in range(k // 512):
        a[p, :8] = np.random.permutation(np.resize(levels, 8))
        for g in range(8):
            far = levels[np.abs(levels - a[p, g]) >= 10]
            a[p, g + 8] = far[np.random.randint(len(far))]
    return np.exp2(a.ravel()).repeat(32)


def f64(x):
    return np.asarray(x).astype(np.float64)


def striped(idx):
    return np.tile(idx.reshape(-1, 16).T, (8, 1)).astype(np.uint16)


def unstriped(offs):
    return offs[:16].T.reshape(-1).astype(np.int64)


def pack_weight(w):
    k, n = w.shape
    w = f64(np.asarray(w, np.float32).astype(ml_dtypes.bfloat16)).reshape(k // 32, 32, n)
    amax = np.abs(w).max(1)
    byte = np.clip(np.where(amax > 0, np.frexp(amax)[1] - 1 + 127 - 7, 1), 1, 254)
    scaled = (w * np.exp2(127.0 - byte)[:, None, :]).reshape(k, n).astype(np.float32)
    words = np.ascontiguousarray(scaled.reshape(k // 512, 128, 4, n).transpose(0, 1, 3, 2)).astype(ml_dtypes.float8_e4m3fn).view(np.uint8)
    return words, np.ascontiguousarray(byte.astype(np.uint8).reshape(k // 512, 16, n))


def unpack_weight(words, scales):
    g, p, n, _ = words.shape
    vals = np.ascontiguousarray(words).view(ml_dtypes.float8_e4m3fn).astype(np.float64) * np.repeat(np.exp2(scales.astype(np.float64) - 127.0), 8, axis=1)[..., None]
    return vals.transpose(0, 1, 3, 2).reshape(g * 512, n)


E2M1 = np.array([0.0, 0.5, 1.0, 1.5, 2.0, 3.0, 4.0, 6.0, -0.0, -0.5, -1.0, -1.5, -2.0, -3.0, -4.0, -6.0])


def pack_fp4(w):
    k, n = w.shape
    w = f64(np.asarray(w, np.float32).astype(ml_dtypes.bfloat16)).reshape(k // 32, 32, n)
    amax = np.abs(w).max(1)
    mant, ex = np.frexp(amax / 6.0)
    byte = np.clip(np.where(amax > 0, np.where(mant > 0.5, ex, ex - 1) + 127, 1), 1, 254)
    scaled = (w * np.exp2(127.0 - byte)[:, None, :]).reshape(k, n).astype(np.float32)
    c = np.ascontiguousarray(scaled.reshape(k // 512, 128, 4, n).transpose(0, 1, 3, 2)).astype(ml_dtypes.float4_e2m1fn).view(np.uint8) & 0xF
    words = (c[..., 0::2] | (c[..., 1::2] << 4)).reshape(k // 512, 128, 2 * n)
    return np.ascontiguousarray(words), np.ascontiguousarray(byte.astype(np.uint8).reshape(k // 512, 16, n))


def unpack_fp4(words, scales):
    g, _, n = scales.shape
    words = np.ascontiguousarray(words).reshape(g, 128, n, 2)
    nib = np.empty((g, 128, n, 4), np.uint8)
    nib[..., 0::2] = words & 0xF
    nib[..., 1::2] = words >> 4
    vals = E2M1[nib] * np.repeat(np.exp2(scales.astype(np.float64) - 127.0), 8, axis=1)[..., None]
    return vals.transpose(0, 1, 3, 2).reshape(g * 512, n)


def sigmoid(v):
    return 1.0 / (1.0 + np.exp(-np.maximum(v, -700.0)))


K, T, S, N, H, U = 1024, 1024, 512, 256, 512, 1024


def setup_inputs():
    n = np.random.standard_normal
    s = mx_kscale(K)[:, None]
    u = mx_kscale(H)
    packed_xT = pack_weight(n((K, T)) * s)
    packed_w1 = pack_fp4(n((K, H)) / np.sqrt(K) / s)
    packed_w2 = pack_fp4(n((K, H)) / np.sqrt(K) / s)
    packed_w3 = pack_fp4(n((H, N)) / np.sqrt(H) / u[:, None])
    return {
        "x_words": packed_xT[0],
        "x_scales": packed_xT[1],
        "w1_words": packed_w1[0],
        "w1_scales": packed_w1[1],
        "w2_words": packed_w2[0],
        "w2_scales": packed_w2[1],
        "g0": (np.random.uniform(0.3, 1.5, (H, U))).astype(np.float32),
        "cap": (np.random.uniform(0.8, 1.6, (H, U))).astype(np.float32),
        "unit": (np.random.uniform(0.6, 1.4, (H, 1)) * u[:, None]).astype(np.float32),
        "w3_words": packed_w3[0],
        "w3_scales": packed_w3[1],
        "offs": striped(np.random.permutation(T)[:S]),
        "m1": striped(np.random.permutation(np.concatenate([np.arange(S), np.random.randint(0, S, U - S)]))),
        "m2": striped(np.random.permutation(np.concatenate([np.arange(S), np.random.randint(0, S, U - S)]))),
    }


def reference(x_words, x_scales, w1_words, w1_scales, w2_words, w2_scales, g0, cap, unit, w3_words, w3_scales, offs, m1, m2):
    xq = unpack_weight(x_words, x_scales)[:, unstriped(offs)]
    y = unpack_fp4(w1_words, w1_scales).T @ xq
    a1 = y[:, unstriped(m1)]
    a2 = y[:, unstriped(m2)]
    ep = unpack_fp4(w2_words, w2_scales).T @ xq
    e1 = ep[:, unstriped(m1)]
    e2 = ep[:, unstriped(m2)]
    epi = e1 * e2
    ddg = a1 + a2 + 0.7 * epi
    fold = sigmoid(f64(g0) - ddg)
    acr = np.minimum(np.exp(-1.0 * ddg), f64(cap))
    hid = f64(unit) * (fold - (0.4 * np.log(acr + 0.2)))
    return unpack_fp4(w3_words, w3_scales).T @ mxq(hid, 0, "e4m3")

@@ -1,0 +1,283 @@
+import math
+from contextlib import ExitStack
+
+import concourse.mybir as mybir
+from concourse.masks import make_identity
+
+F32 = mybir.dt.float32
+BF16 = mybir.dt.bfloat16
+I32 = mybir.dt.int32
+U32 = mybir.dt.uint32
+U16 = mybir.dt.uint16
+U8 = mybir.dt.uint8
+FP8X4 = mybir.dt.float8_e4m3fn_x4
+FP4X4 = mybir.dt.float4_e2m1fn_x4
+ACT = mybir.ActivationFunctionType
+ALU = mybir.AluOpType
+
+K, T, S, H, N, U = 1024, 1024, 512, 512, 256, 1024
+P = 128
+PACK = 4
+PASSES = K // (P * PACK)
+W = 512
+HALVES = U // W
+SPARE = 16
+BLOCKS = W // P
+LN_SCALE = math.exp(-1.25)
+HYBRID = True
+DEFER = [1,3,5,7]
+CHAIN3 = [2,5]
+
+FLOPS = 2 * 2 * K * H * S + 2 * H * N * U
+
+
+def tile_picked_ymetmu_log_p_kernel(
+    tc, x_words, x_scales, w1_words, w1_scales, w2_words, w2_scales, g0, cap, unit, w3_words, w3_scales, offs, m1, m2, out
+):
+    nc = tc.nc
+    with ExitStack() as ctx:
+        keep = ctx.enter_context(tc.tile_pool(name="keep", bufs=1))
+        ring = ctx.enter_context(tc.tile_pool(name="ring", bufs=3))
+        psum = ctx.enter_context(tc.psum_pool(name="psum", bufs=1))
+
+        offs_sb = keep.tile([P, S // 16], U16, name="offs_sb")
+        m1_sb = keep.tile([P, U // 16], U16, name="m1_sb")
+        m2_sb = keep.tile([P, U // 16], U16, name="m2_sb")
+        xw = [keep.tile([P, T], I32, name=f"xw{o}", tag=f"slot{o}", align_bytes=64) for o in range(PASSES)]
+        xs = keep.tile([P, PASSES, T], U8, name="xs", tag="slot2", align_bytes=64)
+        ww = keep.tile([P, 2, PASSES, 2 * H], U8, name="ww", tag="slot3", align_bytes=64)
+        ws = keep.tile([P, 2, PASSES, H], U8, name="ws", tag="slot4", align_bytes=64)
+
+        nc.vector.memset(xs[:].bitcast(I32), 0)
+        nc.gpsimd.memset(ws[:].bitcast(I32), 0)
+
+        def load_scales(queue, dst, src):
+            for q in range(4):
+                queue.dma_start(
+                    out=dst[32 * q : 32 * q + 4, :, :].bitcast(I32),
+                    in_=src[:, 4 * q : 4 * q + 4, :].rearrange("o q c -> q o c").bitcast(I32),
+                )
+
+        nc.sync.dma_start(offs_sb[:], offs)
+        nc.sync.dma_start(out=xw[0][:], in_=x_words[0].rearrange("p n t -> p (n t)").bitcast(I32))
+        load_scales(nc.sync, xs[:], x_scales)
+        nc.sync.dma_start(out=xw[1][:], in_=x_words[1].rearrange("p n t -> p (n t)").bitcast(I32))
+        for a, (words, scales) in enumerate(((w2_words, w2_scales), (w1_words, w1_scales))):
+            nc.sync.dma_start(out=ww[:, a].bitcast(I32), in_=words.rearrange("o p c -> p o c").bitcast(I32))
+            load_scales(nc.gpsimd if a == 0 else nc.sync, ws[:, a], scales)
+        nc.sync.dma_start(m1_sb[:], m1)
+        nc.sync.dma_start(m2_sb[:], m2)
+        g0_rows = g0.rearrange("(p t) r -> p t r", t=PACK)
+        cap_rows = cap.rearrange("(p t) r -> p t r", t=PACK)
+
+        if HYBRID:
+            ident = keep.tile([P, P], F32, name="ident")
+            make_identity(nc, ident[:])
+
+        y_tab = [keep.tile([P, S + SPARE], F32, name=f"y_tab{t}") for t in range(PACK)]
+        ep_tab = [keep.tile([P, S + SPARE], F32, name=f"ep_tab{t}") for t in range(PACK)]
+        for tab in y_tab + ep_tab:
+            nc.gpsimd.memset(tab[:, S:], 0.0)
+
+        xq_w = [keep.tile([P, S], U32, name=f"xq_w{o}", align_bytes=64) for o in range(PASSES)]
+        xq_s = [keep.tile([P, S], U8, name=f"xq_s{o}", align_bytes=64) for o in range(PASSES)]
+        dealt_w = [keep.tile([P, 2 * PASSES, 2 * P], U8, name=f"dealt_w{t}", tag=f"dealt{t}", align_bytes=64) for t in range(PACK)]
+        dealt_s = [keep.tile([P, 2 * PASSES, P], U8, name=f"dealt_s{t}", align_bytes=64) for t in range(PACK)]
+
+        def deal(t):
+            nc.vector.tensor_copy(
+                out=dealt_w[t][:].bitcast(U16),
+                in_=ww[:].bitcast(U16).rearrange("p a o (m t) -> p t (a o) m", t=PACK)[:, t],
+            )
+            nc.vector.tensor_copy(out=dealt_s[t][:], in_=ws[:].rearrange("p a o (m t) -> p t (a o) m", t=PACK)[:, t])
+
+        for o in range(PASSES):
+            nc.vector.tensor_copy(xq_w[o][:], xw[o][:].bitcast(U32).indirect(offs_sb[:]))
+            nc.vector.tensor_copy(xq_s[o][:], xs[:, o, :].indirect(offs_sb[:]))
+            if o == 0:
+                deal(0)
+        for t in range(1, PACK):
+            deal(t)
+
+        g0_sb, cap_sb = {}, {}
+
+        def load_rows(t):
+            g0_sb[t] = keep.tile([P, U], F32, name=f"g0_{t}", tag=f"slot{t % 2}", align_bytes=64)
+            nc.sync.dma_start(out=g0_sb[t][:], in_=g0_rows[:, t, :])
+            cap_sb[t] = keep.tile([P, U], F32, name=f"cap_{t}", tag=f"slot{2 + t}" if t < 2 else f"dealt{t - 2}", align_bytes=64)
+            nc.sync.dma_start(out=cap_sb[t][:], in_=cap_rows[:, t, :])
+
+        load_rows(0)
+        load_rows(1)
+        unit_sb = keep.tile([P, PACK], F32, name="unit_sb", tag="slot4", align_bytes=64)
+        nc.sync.dma_start(out=unit_sb[:], in_=unit.rearrange("(p t) one -> p (t one)", t=PACK))
+        half_unit = keep.tile([P, PACK], F32, name="half_unit")
+        nc.vector.tensor_scalar(out=half_unit[:], in0=unit_sb[:], scalar1=0.5, scalar2=None, op0=ALU.mult)
+
+        w3w = keep.tile([P, 2 * N], U8, name="w3w", tag="slot4", align_bytes=64)
+        nc.sync.dma_start(out=w3w[:].bitcast(I32), in_=w3_words[0].bitcast(I32))
+
+        def products(t):
+            for a, (tab, sign) in enumerate(((ep_tab[t], 1.0), (y_tab[t], -1.0))):
+                acc = psum.tile([P, S], F32, name="acc", tag="acc", bufs=3)
+                for o in range(PASSES):
+                    g = a * PASSES + o
+                    nc.tensor.matmul_mx(
+                        out=acc[:],
+                        lhsT=dealt_w[t][:, g, :].bitcast(FP4X4),
+                        lhsT_scale=dealt_s[t][:, g, :],
+                        rhs=xq_w[o][:].bitcast(FP8X4),
+                        rhs_scale=xq_s[o][:],
+                        start=(o == 0),
+                        stop=(o == PASSES - 1),
+                    )
+                nc.scalar.activation(out=tab[:, :S], in_=acc[:], func=ACT.Copy, scale=sign)
+
+        chunks = [(t, h) for t in range(PACK) for h in range(HALVES)]
+        last = len(chunks) - 1
+        acr = [keep.tile([P, W], F32, name=f"acr{c}") for c in range(len(chunks))]
+        tanh_out = {}
+        neg_ddg = {}
+        parts = {}
+        boltz = {}
+        back = {}
+
+        def gathers(c):
+            t, h = chunks[c]
+            list1 = m1_sb[:, h * W // 16 : (h + 1) * W // 16]
+            list2 = m2_sb[:, h * W // 16 : (h + 1) * W // 16]
+            e1 = ring.tile([P, W], F32, name="e1")
+            nc.scalar.activation(out=e1[:], in_=ep_tab[t][:].indirect(list1), func=ACT.Copy, scale=-0.7)
+            epi = ring.tile([P, W], F32, name="epi")
+            singles = ring.tile([P, W], F32, name="singles")
+            if c in CHAIN3:
+                nc.vector.tensor_tensor(epi[:], ep_tab[t][:].indirect(list2), e1[:], ALU.mult)
+                nc.vector.tensor_tensor(singles[:], y_tab[t][:].indirect(list1), epi[:], ALU.add)
+            else:
+                a1 = ring.tile([P, W], F32, name="a1")
+                nc.scalar.activation(out=a1[:], in_=y_tab[t][:].indirect(list1), func=ACT.Copy)
+                nc.vector.tensor_tensor(epi[:], ep_tab[t][:].indirect(list2), e1[:], ALU.mult)
+                nc.vector.tensor_tensor(singles[:], y_tab[t][:].indirect(list2), a1[:], ALU.add)
+            parts[c] = (epi, singles, list2)
+
+        def close(c):
+            t, h = chunks[c]
+            epi, singles, list2 = parts[c]
+            neg_ddg[c] = ring.tile([P, W], F32, name="neg_ddg")
+            if c in CHAIN3:
+                nc.vector.tensor_tensor(neg_ddg[c][:], y_tab[t][:].indirect(list2), singles[:], ALU.add)
+            else:
+                nc.vector.tensor_tensor(neg_ddg[c][:], epi[:], singles[:], ALU.add)
+
+        def turn_back(c, bank):
+            for b in range(BLOCKS):
+                cols = slice(b * P, (b + 1) * P)
+                nc.tensor.transpose(bank[:, cols], tanh_out[c][:, cols], ident[:])
+            back[c] = bank
+
+        def functions(c):
+            t, h = chunks[c]
+            boltz[c] = keep.tile([P, W], F32, name=f"boltz{c}")
+            nc.scalar.activation(out=boltz[c][:], in_=neg_ddg[c][:], func=ACT.Exp)
+            if HYBRID:
+                z = psum.tile([P, W], F32, name="z", tag="z", bufs=2)
+                for b in range(BLOCKS):
+                    cols = slice(b * P, (b + 1) * P)
+                    src = g0_sb[t][:, h * W + b * P : h * W + (b + 1) * P]
+                    nc.tensor.matmul(z[:, cols], src, ident[:], is_transpose=True, start=True, stop=False)
+                    nc.tensor.matmul(z[:, cols], neg_ddg[c][:, cols], ident[:], is_transpose=True, start=False, stop=True)
+                tanh_out[c] = keep.tile([P, W], F32, name=f"tanh{c}", tag="late" if c == last else f"tanh{c}")
+            else:
+                z = keep.tile([P, W], F32, name=f"z{c}", tag="late" if c == last else f"z{c % 3}")
+                nc.vector.tensor_tensor(z[:], neg_ddg[c][:], g0_sb[t][:, h * W : (h + 1) * W], ALU.add)
+                tanh_out[c] = keep.tile([P, W], F32, name=f"tanh{c}")
+            nc.scalar.activation(out=tanh_out[c][:], in_=z[:], func=ACT.Tanh, scale=0.5)
+            if HYBRID and c == last:
+                turn_back(c, psum.tile([P, W], F32, name="held", tag="held"))
+
+        def capped(c):
+            t, h = chunks[c]
+            nc.vector.tensor_tensor(acr[c][:], boltz[c][:], cap_sb[t][:, h * W : (h + 1) * W], ALU.min)
+
+        products(0)
+        for step in range(len(chunks) + 1):
+            if step < len(chunks):
+                gathers(step)
+            if step >= 2 and step - 2 not in DEFER:
+                capped(step - 2)
+            if step < len(chunks):
+                close(step)
+                if step % HALVES == 0 and step // HALVES + 1 < PACK:
+                    products(step // HALVES + 1)
+            if step >= 1:
+                functions(step - 1)
+                if step % HALVES == 0 and step // HALVES + 1 < PACK:
+                    load_rows(step // HALVES + 1)
+        for c in DEFER:
+            capped(c)
+
+        w3s = keep.tile([P, N], U8, name="w3s", tag="slot0", align_bytes=64)
+        nc.gpsimd.memset(w3s[:].bitcast(I32), 0)
+        for q in range(4):
+            nc.sync.dma_start(out=w3s[32 * q : 32 * q + 4, :].bitcast(I32), in_=w3_scales[0, 4 * q : 4 * q + 4, :].bitcast(I32))
+
+        logs = keep.tile([P, len(chunks), W], F32, name="logs", tag="late")
+        summed = [keep.tile([P, PACK, W], F32, name=f"summed{h}") for h in range(HALVES)]
+
+        def combine(t, h):
+            c = t * HALVES + h
+            nc.scalar.activation(out=logs[:, c, :], in_=acr[c][:], func=ACT.Ln, scale=LN_SCALE, bias=0.2 * LN_SCALE)
+            if HYBRID:
+                if c != last:
+                    turn_back(c, psum.tile([P, W], F32, name="back", tag="back", bufs=2))
+                folded = back[c]
+            else:
+                folded = tanh_out[c]
+            nc.vector.scalar_tensor_tensor(
+                out=summed[h][:, t, :], in0=logs[:, c, :], scalar=-0.8, in1=folded[:], op0=ALU.mult, op1=ALU.add
+            )
+
+        def finish(h, j, width):
+            cols = slice(j * width, (j + 1) * width)
+            hid = keep.tile([P, width * PACK], BF16, name=f"hid{h}_{j}", align_bytes=64)
+            nc.vector.tensor_tensor(
+                hid[:].rearrange("p (c i t) -> p c t i", i=4, t=PACK),
+                summed[h][:, :, cols].rearrange("p t (c i) -> p c t i", i=4),
+                half_unit[:].unsqueeze(1).unsqueeze(3).broadcast_to([P, width // 4, PACK, 4]),
+                ALU.mult,
+            )
+            return hid
+
+        def last_product(h, j, width, hid):
+            codes = keep.tile([P, width], U32, name=f"codes{h}_{j}", align_bytes=64)
+            scales = keep.tile([P, width], U8, name=f"scales{h}_{j}", align_bytes=64)
+            nc.vector.quantize_mx(out=codes[:].bitcast(FP8X4), scales=scales[:], in_=hid[:])
+            for m in range(N // P):
+                acc = psum.tile([P, width], F32, name="acc", tag="acc", bufs=3)
+                nc.tensor.matmul_mx(
+                    out=acc[:],
+                    lhsT=w3w[:, 2 * m * P : 2 * (m + 1) * P].bitcast(FP4X4),
+                    lhsT_scale=w3s[:, m * P : (m + 1) * P],
+                    rhs=codes[:].bitcast(FP8X4),
+                    rhs_scale=scales[:],
+                    start=True,
+                    stop=True,
+                )
+                result = keep.tile([P, width], F32, name=f"result{h}_{j}_{m}")
+                if h == HALVES - 1 and j == W // width - 1 and m == 1:
+                    nc.vector.tensor_copy(out=result[:], in_=acc[:])
+                else:
+                    nc.scalar.copy(out=result[:], in_=acc[:])
+                nc.sync.dma_start(out=out[m * P : (m + 1) * P, h * W + j * width : h * W + (j + 1) * width], in_=result[:])
+
+        for t in range(PACK):
+            combine(t, 0)
+        combine(0, 1)
+        hid = finish(0, 0, W)
+        combine(1, 1)
+        last_product(0, 0, W, hid)
+        combine(2, 1)
+        combine(3, 1)
+        hids = [finish(1, j, W // 2) for j in range(2)]
+        for j in range(2):
+            last_product(1, j, W // 2, hids[j])

@@ -25,8 +25,8 @@ SPARE = 16
 BLOCKS = W // P
 LN_SCALE = math.exp(-1.25)
 HYBRID = True
-DEFER = [1,3,5,7]
-CHAIN3 = [2,5]
+DEFER = [4,6,1,3,5,7]
+CHAIN3 = [0,4]
 
 FLOPS = 2 * 2 * K * H * S + 2 * H * N * U
 
@@ -37,7 +37,7 @@ def tile_picked_ymetmu_log_p_kernel(
     nc = tc.nc
     with ExitStack() as ctx:
         keep = ctx.enter_context(tc.tile_pool(name="keep", bufs=1))
-        ring = ctx.enter_context(tc.tile_pool(name="ring", bufs=3))
+        ring = ctx.enter_context(tc.tile_pool(name="ring", bufs=4))
         psum = ctx.enter_context(tc.psum_pool(name="psum", bufs=1))
 
         offs_sb = keep.tile([P, S // 16], U16, name="offs_sb")
@@ -64,7 +64,7 @@ def tile_picked_ymetmu_log_p_kernel(
         nc.sync.dma_start(out=xw[1][:], in_=x_words[1].rearrange("p n t -> p (n t)").bitcast(I32))
         for a, (words, scales) in enumerate(((w2_words, w2_scales), (w1_words, w1_scales))):
             nc.sync.dma_start(out=ww[:, a].bitcast(I32), in_=words.rearrange("o p c -> p o c").bitcast(I32))
-            load_scales(nc.gpsimd if a == 0 else nc.sync, ws[:, a], scales)
+            load_scales(nc.sync, ws[:, a], scales)
         nc.sync.dma_start(m1_sb[:], m1)
         nc.sync.dma_start(m2_sb[:], m2)
         g0_rows = g0.rearrange("(p t) r -> p t r", t=PACK)
@@ -84,18 +84,17 @@ def tile_picked_ymetmu_log_p_kernel(
         dealt_w = [keep.tile([P, 2 * PASSES, 2 * P], U8, name=f"dealt_w{t}", tag=f"dealt{t}", align_bytes=64) for t in range(PACK)]
         dealt_s = [keep.tile([P, 2 * PASSES, P], U8, name=f"dealt_s{t}", align_bytes=64) for t in range(PACK)]
 
-        def deal(t):
+        def deal(t, groups=slice(0, 2 * PASSES)):
             nc.vector.tensor_copy(
-                out=dealt_w[t][:].bitcast(U16),
-                in_=ww[:].bitcast(U16).rearrange("p a o (m t) -> p t (a o) m", t=PACK)[:, t],
+                out=dealt_w[t][:, groups, :].bitcast(U16),
+                in_=ww[:].bitcast(U16).rearrange("p a o (m t) -> p t (a o) m", t=PACK)[:, t, groups, :],
             )
-            nc.vector.tensor_copy(out=dealt_s[t][:], in_=ws[:].rearrange("p a o (m t) -> p t (a o) m", t=PACK)[:, t])
+            nc.vector.tensor_copy(out=dealt_s[t][:, groups, :], in_=ws[:].rearrange("p a o (m t) -> p t (a o) m", t=PACK)[:, t, groups, :])
 
         for o in range(PASSES):
             nc.vector.tensor_copy(xq_w[o][:], xw[o][:].bitcast(U32).indirect(offs_sb[:]))
             nc.vector.tensor_copy(xq_s[o][:], xs[:, o, :].indirect(offs_sb[:]))
-            if o == 0:
-                deal(0)
+            deal(0, slice(o * PASSES, (o + 1) * PASSES))
         for t in range(1, PACK):
             deal(t)
 
@@ -112,7 +111,7 @@ def tile_picked_ymetmu_log_p_kernel(
         unit_sb = keep.tile([P, PACK], F32, name="unit_sb", tag="slot4", align_bytes=64)
         nc.sync.dma_start(out=unit_sb[:], in_=unit.rearrange("(p t) one -> p (t one)", t=PACK))
         half_unit = keep.tile([P, PACK], F32, name="half_unit")
-        nc.vector.tensor_scalar(out=half_unit[:], in0=unit_sb[:], scalar1=0.5, scalar2=None, op0=ALU.mult)
+        nc.gpsimd.tensor_scalar(out=half_unit[:], in0=unit_sb[:], scalar1=0.5, scalar2=0.0, op0=ALU.mult, op1=ALU.add)
 
         w3w = keep.tile([P, 2 * N], U8, name="w3w", tag="slot4", align_bytes=64)
         nc.sync.dma_start(out=w3w[:].bitcast(I32), in_=w3_words[0].bitcast(I32))
@@ -131,11 +130,14 @@ def tile_picked_ymetmu_log_p_kernel(
                         start=(o == 0),
                         stop=(o == PASSES - 1),
                     )
-                nc.scalar.activation(out=tab[:, :S], in_=acc[:], func=ACT.Copy, scale=sign)
+                if t == 0 and a == 1:
+                    nc.vector.tensor_scalar(out=tab[:, :S], in0=acc[:], scalar1=sign, scalar2=None, op0=ALU.mult)
+                else:
+                    nc.scalar.activation(out=tab[:, :S], in_=acc[:], func=ACT.Copy, scale=sign)
 
         chunks = [(t, h) for t in range(PACK) for h in range(HALVES)]
         last = len(chunks) - 1
-        acr = [keep.tile([P, W], F32, name=f"acr{c}") for c in range(len(chunks))]
+        acr = {}
         tanh_out = {}
         neg_ddg = {}
         parts = {}
@@ -146,10 +148,13 @@ def tile_picked_ymetmu_log_p_kernel(
             t, h = chunks[c]
             list1 = m1_sb[:, h * W // 16 : (h + 1) * W // 16]
             list2 = m2_sb[:, h * W // 16 : (h + 1) * W // 16]
-            e1 = ring.tile([P, W], F32, name="e1")
+            e1 = keep.tile([P, W], F32, name=f"e1_{c}", tag=f"pair{c}")
             nc.scalar.activation(out=e1[:], in_=ep_tab[t][:].indirect(list1), func=ACT.Copy, scale=-0.7)
             epi = ring.tile([P, W], F32, name="epi")
-            singles = ring.tile([P, W], F32, name="singles")
+            if c == last:
+                singles = keep.tile([P, W], F32, name="singles_last", tag="closing")
+            else:
+                singles = ring.tile([P, W], F32, name="singles")
             if c in CHAIN3:
                 nc.vector.tensor_tensor(epi[:], ep_tab[t][:].indirect(list2), e1[:], ALU.mult)
                 nc.vector.tensor_tensor(singles[:], y_tab[t][:].indirect(list1), epi[:], ALU.add)
@@ -179,42 +184,43 @@ def tile_picked_ymetmu_log_p_kernel(
             t, h = chunks[c]
             boltz[c] = keep.tile([P, W], F32, name=f"boltz{c}")
             nc.scalar.activation(out=boltz[c][:], in_=neg_ddg[c][:], func=ACT.Exp)
-            if HYBRID:
+            if c != last:
                 z = psum.tile([P, W], F32, name="z", tag="z", bufs=2)
                 for b in range(BLOCKS):
                     cols = slice(b * P, (b + 1) * P)
                     src = g0_sb[t][:, h * W + b * P : h * W + (b + 1) * P]
                     nc.tensor.matmul(z[:, cols], src, ident[:], is_transpose=True, start=True, stop=False)
                     nc.tensor.matmul(z[:, cols], neg_ddg[c][:, cols], ident[:], is_transpose=True, start=False, stop=True)
-                tanh_out[c] = keep.tile([P, W], F32, name=f"tanh{c}", tag="late" if c == last else f"tanh{c}")
+                tanh_out[c] = keep.tile([P, W], F32, name=f"tanh{c}")
             else:
                 z = keep.tile([P, W], F32, name=f"z{c}", tag="late" if c == last else f"z{c % 3}")
                 nc.vector.tensor_tensor(z[:], neg_ddg[c][:], g0_sb[t][:, h * W : (h + 1) * W], ALU.add)
                 tanh_out[c] = keep.tile([P, W], F32, name=f"tanh{c}")
             nc.scalar.activation(out=tanh_out[c][:], in_=z[:], func=ACT.Tanh, scale=0.5)
-            if HYBRID and c == last:
-                turn_back(c, psum.tile([P, W], F32, name="held", tag="held"))
 
-        def capped(c):
+        def capped(c, dst):
             t, h = chunks[c]
-            nc.vector.tensor_tensor(acr[c][:], boltz[c][:], cap_sb[t][:, h * W : (h + 1) * W], ALU.min)
+            acr[c] = dst
+            nc.vector.tensor_tensor(acr[c], boltz[c][:], cap_sb[t][:, h * W : (h + 1) * W], ALU.min)
 
         products(0)
-        for step in range(len(chunks) + 1):
+        for step in range(len(chunks) + 2):
             if step < len(chunks):
                 gathers(step)
-            if step >= 2 and step - 2 not in DEFER:
-                capped(step - 2)
+            if 3 <= step <= last and step - 3 not in DEFER:
+                capped(step - 3, keep.tile([P, W], F32, name=f"acr{step - 3}", tag=f"pair{step}")[:])
             if step < len(chunks):
                 close(step)
                 if step % HALVES == 0 and step // HALVES + 1 < PACK:
                     products(step // HALVES + 1)
-            if step >= 1:
-                functions(step - 1)
-                if step % HALVES == 0 and step // HALVES + 1 < PACK:
-                    load_rows(step // HALVES + 1)
-        for c in DEFER:
-            capped(c)
+            if step >= 2:
+                done = step - 2
+                functions(done)
+                if done % HALVES == 1 and done // HALVES + 2 < PACK:
+                    load_rows(done // HALVES + 2)
+        acr_late = keep.tile([P, len(DEFER), W], F32, name="acr_late", tag="closing")
+        for n, c in enumerate(DEFER):
+            capped(c, acr_late[:, n, :])
 
         w3s = keep.tile([P, N], U8, name="w3s", tag="slot0", align_bytes=64)
         nc.gpsimd.memset(w3s[:].bitcast(I32), 0)
@@ -226,10 +232,9 @@ def tile_picked_ymetmu_log_p_kernel(
 
         def combine(t, h):
             c = t * HALVES + h
-            nc.scalar.activation(out=logs[:, c, :], in_=acr[c][:], func=ACT.Ln, scale=LN_SCALE, bias=0.2 * LN_SCALE)
-            if HYBRID:
-                if c != last:
-                    turn_back(c, psum.tile([P, W], F32, name="back", tag="back", bufs=2))
+            nc.scalar.activation(out=logs[:, c, :], in_=acr[c], func=ACT.Ln, scale=LN_SCALE, bias=0.2 * LN_SCALE)
+            if c != last:
+                turn_back(c, psum.tile([P, W], F32, name="back", tag="back", bufs=3))
                 folded = back[c]
             else:
                 folded = tanh_out[c]
@@ -245,6 +250,17 @@ def tile_picked_ymetmu_log_p_kernel(
                 summed[h][:, :, cols].rearrange("p t (c i) -> p c t i", i=4),
                 half_unit[:].unsqueeze(1).unsqueeze(3).broadcast_to([P, width // 4, PACK, 4]),
                 ALU.mult,
+            )
+            return hid
+
+        def finish_two_engines(h):
+            planes = keep.tile([P, PACK, W], BF16, name=f"planes{h}")
+            for t in range(PACK):
+                nc.scalar.activation(out=planes[:, t, :], in_=summed[h][:, t, :], func=ACT.Copy, scale=half_unit[:, t : t + 1])
+            hid = keep.tile([P, W * PACK], BF16, name=f"hid{h}", align_bytes=64)
+            nc.vector.tensor_copy(
+                out=hid[:].rearrange("p (c i t) -> p c t i", i=4, t=PACK),
+                in_=planes[:].rearrange("p t (c i) -> p c t i", i=4),
             )
             return hid
 
@@ -273,11 +289,11 @@ def tile_picked_ymetmu_log_p_kernel(
         for t in range(PACK):
             combine(t, 0)
         combine(0, 1)
-        hid = finish(0, 0, W)
         combine(1, 1)
-        last_product(0, 0, W, hid)
+        hid = finish_two_engines(0)
         combine(2, 1)
         combine(3, 1)
+        last_product(0, 0, W, hid)
         hids = [finish(1, j, W // 2) for j in range(2)]
         for j in range(2):
             last_product(1, j, W // 2, hids[j])

@@ -25,7 +25,8 @@ SPARE = 16
 BLOCKS = W // P
 LN_SCALE = math.exp(-1.25)
 HYBRID = True
-DEFER = [4,6,1,3,5,7]
+DEFER = [2,4,6,1,3,5,7]
+PE_SUM = []
 CHAIN3 = [0,4]
 
 FLOPS = 2 * 2 * K * H * S + 2 * H * N * U
@@ -61,12 +62,12 @@ def tile_picked_ymetmu_log_p_kernel(
         nc.sync.dma_start(offs_sb[:], offs)
         nc.sync.dma_start(out=xw[0][:], in_=x_words[0].rearrange("p n t -> p (n t)").bitcast(I32))
         load_scales(nc.sync, xs[:], x_scales)
+        nc.sync.dma_start(m1_sb[:], m1)
+        nc.sync.dma_start(m2_sb[:], m2)
         nc.sync.dma_start(out=xw[1][:], in_=x_words[1].rearrange("p n t -> p (n t)").bitcast(I32))
         for a, (words, scales) in enumerate(((w2_words, w2_scales), (w1_words, w1_scales))):
             nc.sync.dma_start(out=ww[:, a].bitcast(I32), in_=words.rearrange("o p c -> p o c").bitcast(I32))
             load_scales(nc.sync, ws[:, a], scales)
-        nc.sync.dma_start(m1_sb[:], m1)
-        nc.sync.dma_start(m2_sb[:], m2)
         g0_rows = g0.rearrange("(p t) r -> p t r", t=PACK)
         cap_rows = cap.rearrange("(p t) r -> p t r", t=PACK)
 
@@ -93,6 +94,7 @@ def tile_picked_ymetmu_log_p_kernel(
 
         for o in range(PASSES):
             nc.vector.tensor_copy(xq_w[o][:], xw[o][:].bitcast(U32).indirect(offs_sb[:]))
+        for o in range(PASSES):
             nc.vector.tensor_copy(xq_s[o][:], xs[:, o, :].indirect(offs_sb[:]))
             deal(0, slice(o * PASSES, (o + 1) * PASSES))
         for t in range(1, PACK):
@@ -118,7 +120,7 @@ def tile_picked_ymetmu_log_p_kernel(
 
         def products(t):
             for a, (tab, sign) in enumerate(((ep_tab[t], 1.0), (y_tab[t], -1.0))):
-                acc = psum.tile([P, S], F32, name="acc", tag="acc", bufs=3)
+                acc = psum.tile([P, S], F32, name="acc", tag="acc", bufs=2)
                 for o in range(PASSES):
                     g = a * PASSES + o
                     nc.tensor.matmul_mx(
@@ -144,73 +146,91 @@ def tile_picked_ymetmu_log_p_kernel(
         boltz = {}
         back = {}
 
-        def gathers(c):
+        def first(c):
             t, h = chunks[c]
             list1 = m1_sb[:, h * W // 16 : (h + 1) * W // 16]
             list2 = m2_sb[:, h * W // 16 : (h + 1) * W // 16]
             e1 = keep.tile([P, W], F32, name=f"e1_{c}", tag=f"pair{c}")
             nc.scalar.activation(out=e1[:], in_=ep_tab[t][:].indirect(list1), func=ACT.Copy, scale=-0.7)
             epi = ring.tile([P, W], F32, name="epi")
+            a1 = None
+            if c not in CHAIN3:
+                a1 = ring.tile([P, W], F32, name="a1")
+                nc.scalar.activation(out=a1[:], in_=y_tab[t][:].indirect(list1), func=ACT.Copy)
+            nc.vector.tensor_tensor(epi[:], ep_tab[t][:].indirect(list2), e1[:], ALU.mult)
+            parts[c] = (epi, a1, list1, list2)
+
+        def second(c):
+            t, h = chunks[c]
+            epi, a1, list1, list2 = parts[c]
             if c == last:
                 singles = keep.tile([P, W], F32, name="singles_last", tag="closing")
             else:
                 singles = ring.tile([P, W], F32, name="singles")
             if c in CHAIN3:
-                nc.vector.tensor_tensor(epi[:], ep_tab[t][:].indirect(list2), e1[:], ALU.mult)
                 nc.vector.tensor_tensor(singles[:], y_tab[t][:].indirect(list1), epi[:], ALU.add)
             else:
-                a1 = ring.tile([P, W], F32, name="a1")
-                nc.scalar.activation(out=a1[:], in_=y_tab[t][:].indirect(list1), func=ACT.Copy)
-                nc.vector.tensor_tensor(epi[:], ep_tab[t][:].indirect(list2), e1[:], ALU.mult)
                 nc.vector.tensor_tensor(singles[:], y_tab[t][:].indirect(list2), a1[:], ALU.add)
             parts[c] = (epi, singles, list2)
 
         def close(c):
             t, h = chunks[c]
             epi, singles, list2 = parts[c]
-            neg_ddg[c] = ring.tile([P, W], F32, name="neg_ddg")
+            if c in PE_SUM:
+                return
+            if c == last - 1:
+                neg_ddg[c] = keep.tile([P, W], F32, name="neg_ddg_late", tag="late")
+            else:
+                neg_ddg[c] = ring.tile([P, W], F32, name="neg_ddg")
             if c in CHAIN3:
                 nc.vector.tensor_tensor(neg_ddg[c][:], y_tab[t][:].indirect(list2), singles[:], ALU.add)
             else:
                 nc.vector.tensor_tensor(neg_ddg[c][:], epi[:], singles[:], ALU.add)
 
-        def turn_back(c, bank):
+        def turned_sum(bank, terms):
             for b in range(BLOCKS):
                 cols = slice(b * P, (b + 1) * P)
-                nc.tensor.transpose(bank[:, cols], tanh_out[c][:, cols], ident[:])
-            back[c] = bank
+                for n, term in enumerate(terms):
+                    nc.tensor.matmul(bank[:, cols], term[:, cols], ident[:], is_transpose=True, start=(n == 0), stop=(n == len(terms) - 1))
+            return bank
 
         def functions(c):
             t, h = chunks[c]
+            background = g0_sb[t][:, h * W : (h + 1) * W]
             boltz[c] = keep.tile([P, W], F32, name=f"boltz{c}")
-            nc.scalar.activation(out=boltz[c][:], in_=neg_ddg[c][:], func=ACT.Exp)
-            if c != last:
-                z = psum.tile([P, W], F32, name="z", tag="z", bufs=2)
-                for b in range(BLOCKS):
-                    cols = slice(b * P, (b + 1) * P)
-                    src = g0_sb[t][:, h * W + b * P : h * W + (b + 1) * P]
-                    nc.tensor.matmul(z[:, cols], src, ident[:], is_transpose=True, start=True, stop=False)
-                    nc.tensor.matmul(z[:, cols], neg_ddg[c][:, cols], ident[:], is_transpose=True, start=False, stop=True)
-                tanh_out[c] = keep.tile([P, W], F32, name=f"tanh{c}")
+            if c in PE_SUM:
+                terms = [parts[c][0][:], parts[c][1][:]]
+                total = turned_sum(psum.tile([P, W], F32, name="total", tag="total", bufs=2), terms)
             else:
-                z = keep.tile([P, W], F32, name=f"z{c}", tag="late" if c == last else f"z{c % 3}")
-                nc.vector.tensor_tensor(z[:], neg_ddg[c][:], g0_sb[t][:, h * W : (h + 1) * W], ALU.add)
-                tanh_out[c] = keep.tile([P, W], F32, name=f"tanh{c}")
+                terms = [neg_ddg[c][:]]
+                total = neg_ddg[c]
+            nc.scalar.activation(out=boltz[c][:], in_=total[:], func=ACT.Exp)
+            if c != last:
+                z = turned_sum(psum.tile([P, W], F32, name="z", tag="z", bufs=2), [background] + terms)
+            else:
+                z = keep.tile([P, W], F32, name="z_last", tag="late")
+                nc.vector.tensor_tensor(z[:], neg_ddg[c][:], background, ALU.add)
+            tanh_out[c] = keep.tile([P, W], F32, name=f"tanh{c}")
             nc.scalar.activation(out=tanh_out[c][:], in_=z[:], func=ACT.Tanh, scale=0.5)
 
         def capped(c, dst):
             t, h = chunks[c]
             acr[c] = dst
-            nc.vector.tensor_tensor(acr[c], boltz[c][:], cap_sb[t][:, h * W : (h + 1) * W], ALU.min)
+            ratio = boltz[c]
+            if c in PE_SUM:
+                ratio = turned_sum(psum.tile([P, W], F32, name="back", tag="back", bufs=2), [boltz[c][:]])
+            nc.vector.tensor_tensor(acr[c], ratio[:], cap_sb[t][:, h * W : (h + 1) * W], ALU.min)
 
         products(0)
         for step in range(len(chunks) + 2):
-            if step < len(chunks):
-                gathers(step)
-            if 3 <= step <= last and step - 3 not in DEFER:
-                capped(step - 3, keep.tile([P, W], F32, name=f"acr{step - 3}", tag=f"pair{step}")[:])
-            if step < len(chunks):
-                close(step)
+            if step <= last:
+                first(step)
+            if 1 <= step <= last + 1:
+                if step - 4 >= 0 and step - 4 not in DEFER:
+                    capped(step - 4, keep.tile([P, W], F32, name=f"acr{step - 4}", tag=f"pair{step - 1}")[:])
+                close(step - 1)
+            if step <= last:
+                second(step)
                 if step % HALVES == 0 and step // HALVES + 1 < PACK:
                     products(step // HALVES + 1)
             if step >= 2:
@@ -234,33 +254,29 @@ def tile_picked_ymetmu_log_p_kernel(
             c = t * HALVES + h
             nc.scalar.activation(out=logs[:, c, :], in_=acr[c], func=ACT.Ln, scale=LN_SCALE, bias=0.2 * LN_SCALE)
             if c != last:
-                turn_back(c, psum.tile([P, W], F32, name="back", tag="back", bufs=3))
-                folded = back[c]
+                folded = turned_sum(psum.tile([P, W], F32, name="folded", tag=("total", "back")[t % 2], bufs=2), [tanh_out[c][:]])
             else:
                 folded = tanh_out[c]
             nc.vector.scalar_tensor_tensor(
                 out=summed[h][:, t, :], in0=logs[:, c, :], scalar=-0.8, in1=folded[:], op0=ALU.mult, op1=ALU.add
             )
 
-        def finish(h, j, width):
-            cols = slice(j * width, (j + 1) * width)
-            hid = keep.tile([P, width * PACK], BF16, name=f"hid{h}_{j}", align_bytes=64)
-            nc.vector.tensor_tensor(
-                hid[:].rearrange("p (c i t) -> p c t i", i=4, t=PACK),
-                summed[h][:, :, cols].rearrange("p t (c i) -> p c t i", i=4),
-                half_unit[:].unsqueeze(1).unsqueeze(3).broadcast_to([P, width // 4, PACK, 4]),
-                ALU.mult,
-            )
-            return hid
-
-        def finish_two_engines(h):
+        def scale_planes(h):
             planes = keep.tile([P, PACK, W], BF16, name=f"planes{h}")
             for t in range(PACK):
-                nc.scalar.activation(out=planes[:, t, :], in_=summed[h][:, t, :], func=ACT.Copy, scale=half_unit[:, t : t + 1])
-            hid = keep.tile([P, W * PACK], BF16, name=f"hid{h}", align_bytes=64)
+                if h == 0 or t < 2:
+                    nc.gpsimd.tensor_scalar(
+                        out=planes[:, t, :], in0=summed[h][:, t, :], scalar1=half_unit[:, t : t + 1], scalar2=0.0, op0=ALU.mult, op1=ALU.add
+                    )
+                else:
+                    nc.scalar.activation(out=planes[:, t, :], in_=summed[h][:, t, :], func=ACT.Copy, scale=half_unit[:, t : t + 1])
+            return planes
+
+        def interleave(h, j, width, planes):
+            hid = keep.tile([P, width * PACK], BF16, name=f"hid{h}_{j}", align_bytes=64)
             nc.vector.tensor_copy(
                 out=hid[:].rearrange("p (c i t) -> p c t i", i=4, t=PACK),
-                in_=planes[:].rearrange("p t (c i) -> p c t i", i=4),
+                in_=planes[:, :, j * width : (j + 1) * width].rearrange("p t (c i) -> p c t i", i=4),
             )
             return hid
 
@@ -269,7 +285,10 @@ def tile_picked_ymetmu_log_p_kernel(
             scales = keep.tile([P, width], U8, name=f"scales{h}_{j}", align_bytes=64)
             nc.vector.quantize_mx(out=codes[:].bitcast(FP8X4), scales=scales[:], in_=hid[:])
             for m in range(N // P):
-                acc = psum.tile([P, width], F32, name="acc", tag="acc", bufs=3)
+                if m == 0:
+                    acc = psum.tile([P, width], F32, name="acc", tag="acc", bufs=2)
+                else:
+                    acc = psum.tile([P, width], F32, name="acc", tag="z", bufs=2)
                 nc.tensor.matmul_mx(
                     out=acc[:],
                     lhsT=w3w[:, 2 * m * P : 2 * (m + 1) * P].bitcast(FP4X4),
@@ -280,20 +299,19 @@ def tile_picked_ymetmu_log_p_kernel(
                     stop=True,
                 )
                 result = keep.tile([P, width], F32, name=f"result{h}_{j}_{m}")
-                if h == HALVES - 1 and j == W // width - 1 and m == 1:
+                if h == 1 and m == 1:
                     nc.vector.tensor_copy(out=result[:], in_=acc[:])
                 else:
                     nc.scalar.copy(out=result[:], in_=acc[:])
                 nc.sync.dma_start(out=out[m * P : (m + 1) * P, h * W + j * width : h * W + (j + 1) * width], in_=result[:])
 
-        for t in range(PACK):
-            combine(t, 0)
-        combine(0, 1)
-        combine(1, 1)
-        hid = finish_two_engines(0)
-        combine(2, 1)
-        combine(3, 1)
+        for h in range(HALVES):
+            for t in range(PACK):
+                combine(t, h)
+        hid = interleave(0, 0, W, scale_planes(0))
+        planes = scale_planes(1)
+        hid_a = interleave(1, 0, W // 2, planes)
         last_product(0, 0, W, hid)
-        hids = [finish(1, j, W // 2) for j in range(2)]
-        for j in range(2):
-            last_product(1, j, W // 2, hids[j])
+        hid_b = interleave(1, 1, W // 2, planes)
+        last_product(1, 0, W // 2, hid_a)
+        last_product(1, 1, W // 2, hid_b)

@@ -18,16 +18,18 @@ ALU = mybir.AluOpType
 K, T, S, H, N, U = 1024, 1024, 512, 512, 256, 1024
 P = 128
 PACK = 4
+QUADRANTS = 4
 PASSES = K // (P * PACK)
 W = 512
 HALVES = U // W
+CHUNKS = [(t, h) for t in range(PACK) for h in range(HALVES)]
+LAST = len(CHUNKS) - 1
 SPARE = 16
-BLOCKS = W // P
-LN_SCALE = math.exp(-1.25)
-HYBRID = True
-DEFER = [2,4,6,1,3,5,7]
-PE_SUM = []
-CHAIN3 = [0,4]
+LAG = 2
+RING = LAG + 2
+LOG_SCALE = math.exp(-1.25)
+CHAINED = (0, 4)
+GPSIMD_TILES = 2
 
 FLOPS = 2 * 2 * K * H * S + 2 * H * N * U
 
@@ -38,97 +40,102 @@ def tile_picked_ymetmu_log_p_kernel(
     nc = tc.nc
     with ExitStack() as ctx:
         keep = ctx.enter_context(tc.tile_pool(name="keep", bufs=1))
-        ring = ctx.enter_context(tc.tile_pool(name="ring", bufs=4))
-        psum = ctx.enter_context(tc.psum_pool(name="psum", bufs=1))
+        ring = ctx.enter_context(tc.tile_pool(name="ring", bufs=RING))
+        psum = ctx.enter_context(tc.psum_pool(name="psum", bufs=2))
+
+        def reused(shape, dtype, name, buffer):
+            return keep.tile(shape, dtype, name=name, tag=buffer, align_bytes=64)
 
         offs_sb = keep.tile([P, S // 16], U16, name="offs_sb")
         m1_sb = keep.tile([P, U // 16], U16, name="m1_sb")
         m2_sb = keep.tile([P, U // 16], U16, name="m2_sb")
-        xw = [keep.tile([P, T], I32, name=f"xw{o}", tag=f"slot{o}", align_bytes=64) for o in range(PASSES)]
-        xs = keep.tile([P, PASSES, T], U8, name="xs", tag="slot2", align_bytes=64)
-        ww = keep.tile([P, 2, PASSES, 2 * H], U8, name="ww", tag="slot3", align_bytes=64)
-        ws = keep.tile([P, 2, PASSES, H], U8, name="ws", tag="slot4", align_bytes=64)
+        x_word_sb = [reused([P, T], I32, f"x_word{o}", f"load{o}") for o in range(PASSES)]
+        x_scale_sb = reused([P, PASSES, T], U8, "x_scale", "load2")
+        w_word_sb = reused([P, 2, PASSES, 2 * H], U8, "w_word", "load3")
+        w_scale_sb = reused([P, 2, PASSES, H], U8, "w_scale", "load4")
+        nc.vector.memset(x_scale_sb[:].bitcast(I32), 0)
+        nc.gpsimd.memset(w_scale_sb[:].bitcast(I32), 0)
 
-        nc.vector.memset(xs[:].bitcast(I32), 0)
-        nc.gpsimd.memset(ws[:].bitcast(I32), 0)
-
-        def load_scales(queue, dst, src):
-            for q in range(4):
-                queue.dma_start(
+        def load_scales(dst, src):
+            for q in range(QUADRANTS):
+                nc.sync.dma_start(
                     out=dst[32 * q : 32 * q + 4, :, :].bitcast(I32),
-                    in_=src[:, 4 * q : 4 * q + 4, :].rearrange("o q c -> q o c").bitcast(I32),
+                    in_=src[:, 4 * q : 4 * q + 4, :].rearrange("o r c -> r o c").bitcast(I32),
                 )
 
         nc.sync.dma_start(offs_sb[:], offs)
-        nc.sync.dma_start(out=xw[0][:], in_=x_words[0].rearrange("p n t -> p (n t)").bitcast(I32))
-        load_scales(nc.sync, xs[:], x_scales)
+        nc.sync.dma_start(out=x_word_sb[0][:], in_=x_words[0].rearrange("p n j -> p (n j)").bitcast(I32))
+        load_scales(x_scale_sb[:], x_scales)
         nc.sync.dma_start(m1_sb[:], m1)
         nc.sync.dma_start(m2_sb[:], m2)
-        nc.sync.dma_start(out=xw[1][:], in_=x_words[1].rearrange("p n t -> p (n t)").bitcast(I32))
+        nc.sync.dma_start(out=x_word_sb[1][:], in_=x_words[1].rearrange("p n j -> p (n j)").bitcast(I32))
         for a, (words, scales) in enumerate(((w2_words, w2_scales), (w1_words, w1_scales))):
-            nc.sync.dma_start(out=ww[:, a].bitcast(I32), in_=words.rearrange("o p c -> p o c").bitcast(I32))
-            load_scales(nc.sync, ws[:, a], scales)
-        g0_rows = g0.rearrange("(p t) r -> p t r", t=PACK)
-        cap_rows = cap.rearrange("(p t) r -> p t r", t=PACK)
+            nc.sync.dma_start(out=w_word_sb[:, a].bitcast(I32), in_=words.rearrange("o p c -> p o c").bitcast(I32))
+            load_scales(w_scale_sb[:, a], scales)
 
-        if HYBRID:
-            ident = keep.tile([P, P], F32, name="ident")
-            make_identity(nc, ident[:])
+        ident = keep.tile([P, P], F32, name="ident")
+        make_identity(nc, ident[:])
 
-        y_tab = [keep.tile([P, S + SPARE], F32, name=f"y_tab{t}") for t in range(PACK)]
+        neg_y_tab = [keep.tile([P, S + SPARE], F32, name=f"neg_y_tab{t}") for t in range(PACK)]
         ep_tab = [keep.tile([P, S + SPARE], F32, name=f"ep_tab{t}") for t in range(PACK)]
-        for tab in y_tab + ep_tab:
+        for tab in neg_y_tab + ep_tab:
             nc.gpsimd.memset(tab[:, S:], 0.0)
 
-        xq_w = [keep.tile([P, S], U32, name=f"xq_w{o}", align_bytes=64) for o in range(PASSES)]
-        xq_s = [keep.tile([P, S], U8, name=f"xq_s{o}", align_bytes=64) for o in range(PASSES)]
-        dealt_w = [keep.tile([P, 2 * PASSES, 2 * P], U8, name=f"dealt_w{t}", tag=f"dealt{t}", align_bytes=64) for t in range(PACK)]
-        dealt_s = [keep.tile([P, 2 * PASSES, P], U8, name=f"dealt_s{t}", align_bytes=64) for t in range(PACK)]
+        picked_words = [keep.tile([P, S], U32, name=f"picked_words{o}", align_bytes=64) for o in range(PASSES)]
+        picked_scales = [keep.tile([P, S], U8, name=f"picked_scales{o}", align_bytes=64) for o in range(PASSES)]
+        dealt_words = [reused([P, 2 * PASSES, 2 * P], U8, f"dealt_words{t}", f"dealt{t}") for t in range(PACK)]
+        dealt_scales = [keep.tile([P, 2 * PASSES, P], U8, name=f"dealt_scales{t}", align_bytes=64) for t in range(PACK)]
 
-        def deal(t, groups=slice(0, 2 * PASSES)):
+        def deal(t, groups):
             nc.vector.tensor_copy(
-                out=dealt_w[t][:, groups, :].bitcast(U16),
-                in_=ww[:].bitcast(U16).rearrange("p a o (m t) -> p t (a o) m", t=PACK)[:, t, groups, :],
+                out=dealt_words[t][:, groups, :].bitcast(U16),
+                in_=w_word_sb[:].bitcast(U16).rearrange("p a o (m t) -> p t (a o) m", t=PACK)[:, t, groups, :],
             )
-            nc.vector.tensor_copy(out=dealt_s[t][:, groups, :], in_=ws[:].rearrange("p a o (m t) -> p t (a o) m", t=PACK)[:, t, groups, :])
+            nc.vector.tensor_copy(
+                out=dealt_scales[t][:, groups, :],
+                in_=w_scale_sb[:].rearrange("p a o (m t) -> p t (a o) m", t=PACK)[:, t, groups, :],
+            )
 
         for o in range(PASSES):
-            nc.vector.tensor_copy(xq_w[o][:], xw[o][:].bitcast(U32).indirect(offs_sb[:]))
-        for o in range(PASSES):
-            nc.vector.tensor_copy(xq_s[o][:], xs[:, o, :].indirect(offs_sb[:]))
-            deal(0, slice(o * PASSES, (o + 1) * PASSES))
+            nc.vector.tensor_copy(picked_words[o][:], x_word_sb[o][:].bitcast(U32).indirect(offs_sb[:]))
+        for n in range(2):
+            nc.vector.tensor_copy(picked_scales[n][:], x_scale_sb[:, n, :].indirect(offs_sb[:]))
+            deal(0, slice(n * PASSES, (n + 1) * PASSES))
         for t in range(1, PACK):
-            deal(t)
+            deal(t, slice(0, 2 * PASSES))
 
+        g0_rows = g0.rearrange("(p t) r -> p t r", t=PACK)
+        cap_rows = cap.rearrange("(p t) r -> p t r", t=PACK)
         g0_sb, cap_sb = {}, {}
 
-        def load_rows(t):
-            g0_sb[t] = keep.tile([P, U], F32, name=f"g0_{t}", tag=f"slot{t % 2}", align_bytes=64)
+        def load_g0(t):
+            g0_sb[t] = reused([P, U], F32, f"g0_{t}", f"load{t % 2}")
             nc.sync.dma_start(out=g0_sb[t][:], in_=g0_rows[:, t, :])
-            cap_sb[t] = keep.tile([P, U], F32, name=f"cap_{t}", tag=f"slot{2 + t}" if t < 2 else f"dealt{t - 2}", align_bytes=64)
+
+        def load_cap(t):
+            cap_sb[t] = reused([P, U], F32, f"cap_{t}", ("load2", "load3", "dealt0", "dealt1")[t])
             nc.sync.dma_start(out=cap_sb[t][:], in_=cap_rows[:, t, :])
 
-        load_rows(0)
-        load_rows(1)
-        unit_sb = keep.tile([P, PACK], F32, name="unit_sb", tag="slot4", align_bytes=64)
+        for t in range(2):
+            load_g0(t)
+            load_cap(t)
+        unit_sb = reused([P, PACK], F32, "unit_sb", "load4")
         nc.sync.dma_start(out=unit_sb[:], in_=unit.rearrange("(p t) one -> p (t one)", t=PACK))
         half_unit = keep.tile([P, PACK], F32, name="half_unit")
         nc.gpsimd.tensor_scalar(out=half_unit[:], in0=unit_sb[:], scalar1=0.5, scalar2=0.0, op0=ALU.mult, op1=ALU.add)
-
-        w3w = keep.tile([P, 2 * N], U8, name="w3w", tag="slot4", align_bytes=64)
-        nc.sync.dma_start(out=w3w[:].bitcast(I32), in_=w3_words[0].bitcast(I32))
+        w3_word_sb = reused([P, 2 * N], U8, "w3_word", "load4")
+        nc.sync.dma_start(out=w3_word_sb[:].bitcast(I32), in_=w3_words[0].bitcast(I32))
 
         def products(t):
-            for a, (tab, sign) in enumerate(((ep_tab[t], 1.0), (y_tab[t], -1.0))):
-                acc = psum.tile([P, S], F32, name="acc", tag="acc", bufs=2)
+            for a, (tab, sign) in enumerate(((ep_tab[t], 1.0), (neg_y_tab[t], -1.0))):
+                acc = psum.tile([P, S], F32, name="acc", tag="product")
                 for o in range(PASSES):
-                    g = a * PASSES + o
                     nc.tensor.matmul_mx(
                         out=acc[:],
-                        lhsT=dealt_w[t][:, g, :].bitcast(FP4X4),
-                        lhsT_scale=dealt_s[t][:, g, :],
-                        rhs=xq_w[o][:].bitcast(FP8X4),
-                        rhs_scale=xq_s[o][:],
+                        lhsT=dealt_words[t][:, a * PASSES + o, :].bitcast(FP4X4),
+                        lhsT_scale=dealt_scales[t][:, a * PASSES + o, :],
+                        rhs=picked_words[o][:].bitcast(FP8X4),
+                        rhs_scale=picked_scales[o][:],
                         start=(o == 0),
                         stop=(o == PASSES - 1),
                     )
@@ -137,181 +144,160 @@ def tile_picked_ymetmu_log_p_kernel(
                 else:
                     nc.scalar.activation(out=tab[:, :S], in_=acc[:], func=ACT.Copy, scale=sign)
 
-        chunks = [(t, h) for t in range(PACK) for h in range(HALVES)]
-        last = len(chunks) - 1
-        acr = {}
-        tanh_out = {}
-        neg_ddg = {}
-        parts = {}
-        boltz = {}
-        back = {}
-
-        def first(c):
-            t, h = chunks[c]
-            list1 = m1_sb[:, h * W // 16 : (h + 1) * W // 16]
-            list2 = m2_sb[:, h * W // 16 : (h + 1) * W // 16]
-            e1 = keep.tile([P, W], F32, name=f"e1_{c}", tag=f"pair{c}")
-            nc.scalar.activation(out=e1[:], in_=ep_tab[t][:].indirect(list1), func=ACT.Copy, scale=-0.7)
-            epi = ring.tile([P, W], F32, name="epi")
-            a1 = None
-            if c not in CHAIN3:
-                a1 = ring.tile([P, W], F32, name="a1")
-                nc.scalar.activation(out=a1[:], in_=y_tab[t][:].indirect(list1), func=ACT.Copy)
-            nc.vector.tensor_tensor(epi[:], ep_tab[t][:].indirect(list2), e1[:], ALU.mult)
-            parts[c] = (epi, a1, list1, list2)
-
-        def second(c):
-            t, h = chunks[c]
-            epi, a1, list1, list2 = parts[c]
-            if c == last:
-                singles = keep.tile([P, W], F32, name="singles_last", tag="closing")
-            else:
-                singles = ring.tile([P, W], F32, name="singles")
-            if c in CHAIN3:
-                nc.vector.tensor_tensor(singles[:], y_tab[t][:].indirect(list1), epi[:], ALU.add)
-            else:
-                nc.vector.tensor_tensor(singles[:], y_tab[t][:].indirect(list2), a1[:], ALU.add)
-            parts[c] = (epi, singles, list2)
-
-        def close(c):
-            t, h = chunks[c]
-            epi, singles, list2 = parts[c]
-            if c in PE_SUM:
-                return
-            if c == last - 1:
-                neg_ddg[c] = keep.tile([P, W], F32, name="neg_ddg_late", tag="late")
-            else:
-                neg_ddg[c] = ring.tile([P, W], F32, name="neg_ddg")
-            if c in CHAIN3:
-                nc.vector.tensor_tensor(neg_ddg[c][:], y_tab[t][:].indirect(list2), singles[:], ALU.add)
-            else:
-                nc.vector.tensor_tensor(neg_ddg[c][:], epi[:], singles[:], ALU.add)
-
         def turned_sum(bank, terms):
-            for b in range(BLOCKS):
+            for b in range(W // P):
                 cols = slice(b * P, (b + 1) * P)
                 for n, term in enumerate(terms):
-                    nc.tensor.matmul(bank[:, cols], term[:, cols], ident[:], is_transpose=True, start=(n == 0), stop=(n == len(terms) - 1))
+                    nc.tensor.matmul(
+                        bank[:, cols], term[:, cols], ident[:], is_transpose=True, start=(n == 0), stop=(n == len(terms) - 1)
+                    )
             return bank
 
+        def offsets(list_sb, c):
+            h = CHUNKS[c][1]
+            return list_sb[:, h * W // 16 : (h + 1) * W // 16]
+
+        def columns(rows_sb, c):
+            t, h = CHUNKS[c]
+            return rows_sb[t][:, h * W : (h + 1) * W]
+
+        neg_epi, neg_a1, partial, neg_ddg, boltz, tanh_sb, acr = {}, {}, {}, {}, {}, {}, {}
+
+        def gather_first(c):
+            t = CHUNKS[c][0]
+            neg_e1 = reused([P, W], F32, f"neg_e1_{c}", f"chunk{c}")
+            nc.scalar.activation(out=neg_e1[:], in_=ep_tab[t][:].indirect(offsets(m1_sb, c)), func=ACT.Copy, scale=-0.7)
+            neg_epi[c] = ring.tile([P, W], F32, name="neg_epi")
+            if c not in CHAINED:
+                neg_a1[c] = ring.tile([P, W], F32, name="neg_a1")
+                nc.scalar.activation(out=neg_a1[c][:], in_=neg_y_tab[t][:].indirect(offsets(m1_sb, c)), func=ACT.Copy)
+            nc.vector.tensor_tensor(neg_epi[c][:], ep_tab[t][:].indirect(offsets(m2_sb, c)), neg_e1[:], ALU.mult)
+
+        def gather_second(c):
+            t = CHUNKS[c][0]
+            if c == LAST:
+                partial[c] = reused([P, W], F32, "partial_last", "after_gathers")
+            else:
+                partial[c] = ring.tile([P, W], F32, name="partial")
+            if c in CHAINED:
+                nc.vector.tensor_tensor(partial[c][:], neg_y_tab[t][:].indirect(offsets(m1_sb, c)), neg_epi[c][:], ALU.add)
+            else:
+                nc.vector.tensor_tensor(partial[c][:], neg_y_tab[t][:].indirect(offsets(m2_sb, c)), neg_a1[c][:], ALU.add)
+
+        def close(c):
+            t = CHUNKS[c][0]
+            if c == LAST - 1:
+                neg_ddg[c] = reused([P, W], F32, "neg_ddg_late", "before_logs")
+            else:
+                neg_ddg[c] = ring.tile([P, W], F32, name="neg_ddg")
+            if c in CHAINED:
+                nc.vector.tensor_tensor(neg_ddg[c][:], neg_y_tab[t][:].indirect(offsets(m2_sb, c)), partial[c][:], ALU.add)
+            else:
+                nc.vector.tensor_tensor(neg_ddg[c][:], neg_epi[c][:], partial[c][:], ALU.add)
+
         def functions(c):
-            t, h = chunks[c]
-            background = g0_sb[t][:, h * W : (h + 1) * W]
             boltz[c] = keep.tile([P, W], F32, name=f"boltz{c}")
-            if c in PE_SUM:
-                terms = [parts[c][0][:], parts[c][1][:]]
-                total = turned_sum(psum.tile([P, W], F32, name="total", tag="total", bufs=2), terms)
+            nc.scalar.activation(out=boltz[c][:], in_=neg_ddg[c][:], func=ACT.Exp)
+            if c != LAST:
+                margin = turned_sum(psum.tile([P, W], F32, name="margin", tag="margin"), [columns(g0_sb, c), neg_ddg[c][:]])
             else:
-                terms = [neg_ddg[c][:]]
-                total = neg_ddg[c]
-            nc.scalar.activation(out=boltz[c][:], in_=total[:], func=ACT.Exp)
-            if c != last:
-                z = turned_sum(psum.tile([P, W], F32, name="z", tag="z", bufs=2), [background] + terms)
-            else:
-                z = keep.tile([P, W], F32, name="z_last", tag="late")
-                nc.vector.tensor_tensor(z[:], neg_ddg[c][:], background, ALU.add)
-            tanh_out[c] = keep.tile([P, W], F32, name=f"tanh{c}")
-            nc.scalar.activation(out=tanh_out[c][:], in_=z[:], func=ACT.Tanh, scale=0.5)
+                margin = reused([P, W], F32, "margin_last", "before_logs")
+                nc.vector.tensor_tensor(margin[:], neg_ddg[c][:], columns(g0_sb, c), ALU.add)
+            tanh_sb[c] = keep.tile([P, W], F32, name=f"tanh{c}")
+            nc.scalar.activation(out=tanh_sb[c][:], in_=margin[:], func=ACT.Tanh, scale=0.5)
 
         def capped(c, dst):
-            t, h = chunks[c]
             acr[c] = dst
-            ratio = boltz[c]
-            if c in PE_SUM:
-                ratio = turned_sum(psum.tile([P, W], F32, name="back", tag="back", bufs=2), [boltz[c][:]])
-            nc.vector.tensor_tensor(acr[c], ratio[:], cap_sb[t][:, h * W : (h + 1) * W], ALU.min)
+            nc.vector.tensor_tensor(dst, boltz[c][:], columns(cap_sb, c), ALU.min)
 
         products(0)
-        for step in range(len(chunks) + 2):
-            if step <= last:
-                first(step)
-            if 1 <= step <= last + 1:
-                if step - 4 >= 0 and step - 4 not in DEFER:
-                    capped(step - 4, keep.tile([P, W], F32, name=f"acr{step - 4}", tag=f"pair{step - 1}")[:])
+        for step in range(len(CHUNKS) + LAG):
+            if step <= LAST:
+                gather_first(step)
+            if step == 2 * LAG:
+                capped(0, reused([P, W], F32, "acr0", f"chunk{step - 1}")[:])
+            if 1 <= step <= LAST + 1:
                 close(step - 1)
-            if step <= last:
-                second(step)
+            if step <= LAST:
+                gather_second(step)
                 if step % HALVES == 0 and step // HALVES + 1 < PACK:
                     products(step // HALVES + 1)
-            if step >= 2:
-                done = step - 2
+            if step >= LAG:
+                done = step - LAG
                 functions(done)
                 if done % HALVES == 1 and done // HALVES + 2 < PACK:
-                    load_rows(done // HALVES + 2)
-        acr_late = keep.tile([P, len(DEFER), W], F32, name="acr_late", tag="closing")
-        for n, c in enumerate(DEFER):
+                    load_g0(done // HALVES + 2)
+                    load_cap(done // HALVES + 2)
+
+        by_halves = [t * HALVES + h for h in range(HALVES) for t in range(PACK)]
+        acr_late = reused([P, LAST, W], F32, "acr_late", "after_gathers")
+        for n, c in enumerate(by_halves[1:]):
             capped(c, acr_late[:, n, :])
 
-        w3s = keep.tile([P, N], U8, name="w3s", tag="slot0", align_bytes=64)
-        nc.gpsimd.memset(w3s[:].bitcast(I32), 0)
-        for q in range(4):
-            nc.sync.dma_start(out=w3s[32 * q : 32 * q + 4, :].bitcast(I32), in_=w3_scales[0, 4 * q : 4 * q + 4, :].bitcast(I32))
+        w3_scale_sb = reused([P, 1, N], U8, "w3_scale", "load0")
+        nc.gpsimd.memset(w3_scale_sb[:].bitcast(I32), 0)
+        load_scales(w3_scale_sb[:], w3_scales)
 
-        logs = keep.tile([P, len(chunks), W], F32, name="logs", tag="late")
+        logs = reused([P, len(CHUNKS), W], F32, "logs", "before_logs")
         summed = [keep.tile([P, PACK, W], F32, name=f"summed{h}") for h in range(HALVES)]
-
-        def combine(t, h):
-            c = t * HALVES + h
-            nc.scalar.activation(out=logs[:, c, :], in_=acr[c], func=ACT.Ln, scale=LN_SCALE, bias=0.2 * LN_SCALE)
-            if c != last:
-                folded = turned_sum(psum.tile([P, W], F32, name="folded", tag=("total", "back")[t % 2], bufs=2), [tanh_out[c][:]])
+        for c in by_halves:
+            t, h = CHUNKS[c]
+            nc.scalar.activation(out=logs[:, c, :], in_=acr[c], func=ACT.Ln, scale=LOG_SCALE, bias=0.2 * LOG_SCALE)
+            if c != LAST:
+                tanh_rows = turned_sum(psum.tile([P, W], F32, name="tanh_rows", tag=f"back{t % 2}"), [tanh_sb[c][:]])
             else:
-                folded = tanh_out[c]
+                tanh_rows = tanh_sb[c]
             nc.vector.scalar_tensor_tensor(
-                out=summed[h][:, t, :], in0=logs[:, c, :], scalar=-0.8, in1=folded[:], op0=ALU.mult, op1=ALU.add
+                out=summed[h][:, t, :], in0=logs[:, c, :], scalar=-0.8, in1=tanh_rows[:], op0=ALU.mult, op1=ALU.add
             )
 
-        def scale_planes(h):
-            planes = keep.tile([P, PACK, W], BF16, name=f"planes{h}")
+        def scaled(h):
+            hid_rows = keep.tile([P, PACK, W], BF16, name=f"hid_rows{h}")
             for t in range(PACK):
-                if h == 0 or t < 2:
+                factor = half_unit[:, t : t + 1]
+                if h == 0 or t < GPSIMD_TILES:
                     nc.gpsimd.tensor_scalar(
-                        out=planes[:, t, :], in0=summed[h][:, t, :], scalar1=half_unit[:, t : t + 1], scalar2=0.0, op0=ALU.mult, op1=ALU.add
+                        out=hid_rows[:, t, :], in0=summed[h][:, t, :], scalar1=factor, scalar2=0.0, op0=ALU.mult, op1=ALU.add
                     )
                 else:
-                    nc.scalar.activation(out=planes[:, t, :], in_=summed[h][:, t, :], func=ACT.Copy, scale=half_unit[:, t : t + 1])
-            return planes
+                    nc.scalar.activation(out=hid_rows[:, t, :], in_=summed[h][:, t, :], func=ACT.Copy, scale=factor)
+            return hid_rows
 
-        def interleave(h, j, width, planes):
-            hid = keep.tile([P, width * PACK], BF16, name=f"hid{h}_{j}", align_bytes=64)
+        def interleaved(hid_rows, first, width):
+            hid = keep.tile([P, width * PACK], BF16, name=f"hid{first}", align_bytes=64)
             nc.vector.tensor_copy(
                 out=hid[:].rearrange("p (c i t) -> p c t i", i=4, t=PACK),
-                in_=planes[:, :, j * width : (j + 1) * width].rearrange("p t (c i) -> p c t i", i=4),
+                in_=hid_rows[:, :, first % W : first % W + width].rearrange("p t (c i) -> p c t i", i=4),
             )
             return hid
 
-        def last_product(h, j, width, hid):
-            codes = keep.tile([P, width], U32, name=f"codes{h}_{j}", align_bytes=64)
-            scales = keep.tile([P, width], U8, name=f"scales{h}_{j}", align_bytes=64)
-            nc.vector.quantize_mx(out=codes[:].bitcast(FP8X4), scales=scales[:], in_=hid[:])
+        def last_product(hid, first, width):
+            codes = keep.tile([P, width], U32, name=f"codes{first}", align_bytes=64)
+            hid_scales = keep.tile([P, width], U8, name=f"hid_scales{first}", align_bytes=64)
+            nc.vector.quantize_mx(out=codes[:].bitcast(FP8X4), scales=hid_scales[:], in_=hid[:])
             for m in range(N // P):
-                if m == 0:
-                    acc = psum.tile([P, width], F32, name="acc", tag="acc", bufs=2)
-                else:
-                    acc = psum.tile([P, width], F32, name="acc", tag="z", bufs=2)
+                acc = psum.tile([P, width], F32, name="out_acc", tag=("product", "margin")[m])
                 nc.tensor.matmul_mx(
                     out=acc[:],
-                    lhsT=w3w[:, 2 * m * P : 2 * (m + 1) * P].bitcast(FP4X4),
-                    lhsT_scale=w3s[:, m * P : (m + 1) * P],
+                    lhsT=w3_word_sb[:, 2 * m * P : 2 * (m + 1) * P].bitcast(FP4X4),
+                    lhsT_scale=w3_scale_sb[:, 0, m * P : (m + 1) * P],
                     rhs=codes[:].bitcast(FP8X4),
-                    rhs_scale=scales[:],
+                    rhs_scale=hid_scales[:],
                     start=True,
                     stop=True,
                 )
-                result = keep.tile([P, width], F32, name=f"result{h}_{j}_{m}")
-                if h == 1 and m == 1:
+                result = keep.tile([P, width], F32, name=f"result{first}_{m}")
+                if first >= W and m == 1:
                     nc.vector.tensor_copy(out=result[:], in_=acc[:])
                 else:
                     nc.scalar.copy(out=result[:], in_=acc[:])
-                nc.sync.dma_start(out=out[m * P : (m + 1) * P, h * W + j * width : h * W + (j + 1) * width], in_=result[:])
+                nc.sync.dma_start(out=out[m * P : (m + 1) * P, first : first + width], in_=result[:])
 
-        for h in range(HALVES):
-            for t in range(PACK):
-                combine(t, h)
-        hid = interleave(0, 0, W, scale_planes(0))
-        planes = scale_planes(1)
-        hid_a = interleave(1, 0, W // 2, planes)
-        last_product(0, 0, W, hid)
-        hid_b = interleave(1, 1, W // 2, planes)
-        last_product(1, 0, W // 2, hid_a)
-        last_product(1, 1, W // 2, hid_b)
+        quarter = W // 2
+        hid_half = interleaved(scaled(0), 0, W)
+        second_rows = scaled(1)
+        hid_third = interleaved(second_rows, W, quarter)
+        last_product(hid_half, 0, W)
+        hid_fourth = interleaved(second_rows, W + quarter, quarter)
+        last_product(hid_third, W, quarter)
+        last_product(hid_fourth, W + quarter, quarter)

import math
from contextlib import ExitStack

import concourse.mybir as mybir
from concourse.masks import make_identity

F32 = mybir.dt.float32
BF16 = mybir.dt.bfloat16
I32 = mybir.dt.int32
U32 = mybir.dt.uint32
U16 = mybir.dt.uint16
U8 = mybir.dt.uint8
FP8X4 = mybir.dt.float8_e4m3fn_x4
FP4X4 = mybir.dt.float4_e2m1fn_x4
ACT = mybir.ActivationFunctionType
ALU = mybir.AluOpType

K, T, S, H, N, U = 1024, 1024, 512, 512, 256, 1024
P = 128
PACK = 4
QUADRANTS = 4
PASSES = K // (P * PACK)
W = 512
HALVES = U // W
CHUNKS = [(t, h) for t in range(PACK) for h in range(HALVES)]
LAST = len(CHUNKS) - 1
SPARE = 16
LAG = 2
RING = LAG + 2
LOG_SCALE = math.exp(-1.25)
CHAINED = (0, 4)
GPSIMD_TILES = 2

FLOPS = 2 * 2 * K * H * S + 2 * H * N * U


def tile_picked_ymetmu_log_p_kernel(
    tc, x_words, x_scales, w1_words, w1_scales, w2_words, w2_scales, g0, cap, unit, w3_words, w3_scales, offs, m1, m2, out
):
    nc = tc.nc
    with ExitStack() as ctx:
        keep = ctx.enter_context(tc.tile_pool(name="keep", bufs=1))
        ring = ctx.enter_context(tc.tile_pool(name="ring", bufs=RING))
        psum = ctx.enter_context(tc.psum_pool(name="psum", bufs=2))

        def reused(shape, dtype, name, buffer):
            return keep.tile(shape, dtype, name=name, tag=buffer, align_bytes=64)

        offs_sb = keep.tile([P, S // 16], U16, name="offs_sb")
        m1_sb = keep.tile([P, U // 16], U16, name="m1_sb")
        m2_sb = keep.tile([P, U // 16], U16, name="m2_sb")
        x_word_sb = [reused([P, T], I32, f"x_word{o}", f"load{o}") for o in range(PASSES)]
        x_scale_sb = reused([P, PASSES, T], U8, "x_scale", "load2")
        w_word_sb = reused([P, 2, PASSES, 2 * H], U8, "w_word", "load3")
        w_scale_sb = reused([P, 2, PASSES, H], U8, "w_scale", "load4")
        nc.vector.memset(x_scale_sb[:].bitcast(I32), 0)
        nc.gpsimd.memset(w_scale_sb[:].bitcast(I32), 0)

        def load_scales(dst, src):
            for q in range(QUADRANTS):
                nc.sync.dma_start(
                    out=dst[32 * q : 32 * q + 4, :, :].bitcast(I32),
                    in_=src[:, 4 * q : 4 * q + 4, :].rearrange("o r c -> r o c").bitcast(I32),
                )

        nc.sync.dma_start(offs_sb[:], offs)
        nc.sync.dma_start(out=x_word_sb[0][:], in_=x_words[0].rearrange("p n j -> p (n j)").bitcast(I32))
        load_scales(x_scale_sb[:], x_scales)
        nc.sync.dma_start(m1_sb[:], m1)
        nc.sync.dma_start(m2_sb[:], m2)
        nc.sync.dma_start(out=x_word_sb[1][:], in_=x_words[1].rearrange("p n j -> p (n j)").bitcast(I32))
        for a, (words, scales) in enumerate(((w2_words, w2_scales), (w1_words, w1_scales))):
            nc.sync.dma_start(out=w_word_sb[:, a].bitcast(I32), in_=words.rearrange("o p c -> p o c").bitcast(I32))
            load_scales(w_scale_sb[:, a], scales)

        ident = keep.tile([P, P], F32, name="ident")
        make_identity(nc, ident[:])

        neg_y_tab = [keep.tile([P, S + SPARE], F32, name=f"neg_y_tab{t}") for t in range(PACK)]
        ep_tab = [keep.tile([P, S + SPARE], F32, name=f"ep_tab{t}") for t in range(PACK)]
        for tab in neg_y_tab + ep_tab:
            nc.gpsimd.memset(tab[:, S:], 0.0)

        picked_words = [keep.tile([P, S], U32, name=f"picked_words{o}", align_bytes=64) for o in range(PASSES)]
        picked_scales = [keep.tile([P, S], U8, name=f"picked_scales{o}", align_bytes=64) for o in range(PASSES)]
        dealt_words = [reused([P, 2 * PASSES, 2 * P], U8, f"dealt_words{t}", f"dealt{t}") for t in range(PACK)]
        dealt_scales = [keep.tile([P, 2 * PASSES, P], U8, name=f"dealt_scales{t}", align_bytes=64) for t in range(PACK)]

        def deal(t, groups):
            nc.vector.tensor_copy(
                out=dealt_words[t][:, groups, :].bitcast(U16),
                in_=w_word_sb[:].bitcast(U16).rearrange("p a o (m t) -> p t (a o) m", t=PACK)[:, t, groups, :],
            )
            nc.vector.tensor_copy(
                out=dealt_scales[t][:, groups, :],
                in_=w_scale_sb[:].rearrange("p a o (m t) -> p t (a o) m", t=PACK)[:, t, groups, :],
            )

        for o in range(PASSES):
            nc.vector.tensor_copy(picked_words[o][:], x_word_sb[o][:].bitcast(U32).indirect(offs_sb[:]))
        for n in range(2):
            nc.vector.tensor_copy(picked_scales[n][:], x_scale_sb[:, n, :].indirect(offs_sb[:]))
            deal(0, slice(n * PASSES, (n + 1) * PASSES))
        for t in range(1, PACK):
            deal(t, slice(0, 2 * PASSES))

        g0_rows = g0.rearrange("(p t) r -> p t r", t=PACK)
        cap_rows = cap.rearrange("(p t) r -> p t r", t=PACK)
        g0_sb, cap_sb = {}, {}

        def load_g0(t):
            g0_sb[t] = reused([P, U], F32, f"g0_{t}", f"load{t % 2}")
            nc.sync.dma_start(out=g0_sb[t][:], in_=g0_rows[:, t, :])

        def load_cap(t):
            cap_sb[t] = reused([P, U], F32, f"cap_{t}", ("load2", "load3", "dealt0", "dealt1")[t])
            nc.sync.dma_start(out=cap_sb[t][:], in_=cap_rows[:, t, :])

        for t in range(2):
            load_g0(t)
            load_cap(t)
        unit_sb = reused([P, PACK], F32, "unit_sb", "load4")
        nc.sync.dma_start(out=unit_sb[:], in_=unit.rearrange("(p t) one -> p (t one)", t=PACK))
        half_unit = keep.tile([P, PACK], F32, name="half_unit")
        nc.gpsimd.tensor_scalar(out=half_unit[:], in0=unit_sb[:], scalar1=0.5, scalar2=0.0, op0=ALU.mult, op1=ALU.add)
        w3_word_sb = reused([P, 2 * N], U8, "w3_word", "load4")
        nc.sync.dma_start(out=w3_word_sb[:].bitcast(I32), in_=w3_words[0].bitcast(I32))

        def products(t):
            for a, (tab, sign) in enumerate(((ep_tab[t], 1.0), (neg_y_tab[t], -1.0))):
                acc = psum.tile([P, S], F32, name="acc", tag="product")
                for o in range(PASSES):
                    nc.tensor.matmul_mx(
                        out=acc[:],
                        lhsT=dealt_words[t][:, a * PASSES + o, :].bitcast(FP4X4),
                        lhsT_scale=dealt_scales[t][:, a * PASSES + o, :],
                        rhs=picked_words[o][:].bitcast(FP8X4),
                        rhs_scale=picked_scales[o][:],
                        start=(o == 0),
                        stop=(o == PASSES - 1),
                    )
                if t == 0 and a == 1:
                    nc.vector.tensor_scalar(out=tab[:, :S], in0=acc[:], scalar1=sign, scalar2=None, op0=ALU.mult)
                else:
                    nc.scalar.activation(out=tab[:, :S], in_=acc[:], func=ACT.Copy, scale=sign)

        def turned_sum(bank, terms):
            for b in range(W // P):
                cols = slice(b * P, (b + 1) * P)
                for n, term in enumerate(terms):
                    nc.tensor.matmul(
                        bank[:, cols], term[:, cols], ident[:], is_transpose=True, start=(n == 0), stop=(n == len(terms) - 1)
                    )
            return bank

        def offsets(list_sb, c):
            h = CHUNKS[c][1]
            return list_sb[:, h * W // 16 : (h + 1) * W // 16]

        def columns(rows_sb, c):
            t, h = CHUNKS[c]
            return rows_sb[t][:, h * W : (h + 1) * W]

        neg_epi, neg_a1, partial, neg_ddg, boltz, tanh_sb, acr = {}, {}, {}, {}, {}, {}, {}

        def gather_first(c):
            t = CHUNKS[c][0]
            neg_e1 = reused([P, W], F32, f"neg_e1_{c}", f"chunk{c}")
            nc.scalar.activation(out=neg_e1[:], in_=ep_tab[t][:].indirect(offsets(m1_sb, c)), func=ACT.Copy, scale=-0.7)
            neg_epi[c] = ring.tile([P, W], F32, name="neg_epi")
            if c not in CHAINED:
                neg_a1[c] = ring.tile([P, W], F32, name="neg_a1")
                nc.scalar.activation(out=neg_a1[c][:], in_=neg_y_tab[t][:].indirect(offsets(m1_sb, c)), func=ACT.Copy)
            nc.vector.tensor_tensor(neg_epi[c][:], ep_tab[t][:].indirect(offsets(m2_sb, c)), neg_e1[:], ALU.mult)

        def gather_second(c):
            t = CHUNKS[c][0]
            if c == LAST:
                partial[c] = reused([P, W], F32, "partial_last", "after_gathers")
            else:
                partial[c] = ring.tile([P, W], F32, name="partial")
            if c in CHAINED:
                nc.vector.tensor_tensor(partial[c][:], neg_y_tab[t][:].indirect(offsets(m1_sb, c)), neg_epi[c][:], ALU.add)
            else:
                nc.vector.tensor_tensor(partial[c][:], neg_y_tab[t][:].indirect(offsets(m2_sb, c)), neg_a1[c][:], ALU.add)

        def close(c):
            t = CHUNKS[c][0]
            if c == LAST - 1:
                neg_ddg[c] = reused([P, W], F32, "neg_ddg_late", "before_logs")
            else:
                neg_ddg[c] = ring.tile([P, W], F32, name="neg_ddg")
            if c in CHAINED:
                nc.vector.tensor_tensor(neg_ddg[c][:], neg_y_tab[t][:].indirect(offsets(m2_sb, c)), partial[c][:], ALU.add)
            else:
                nc.vector.tensor_tensor(neg_ddg[c][:], neg_epi[c][:], partial[c][:], ALU.add)

        def functions(c):
            boltz[c] = keep.tile([P, W], F32, name=f"boltz{c}")
            nc.scalar.activation(out=boltz[c][:], in_=neg_ddg[c][:], func=ACT.Exp)
            if c != LAST:
                margin = turned_sum(psum.tile([P, W], F32, name="margin", tag="margin"), [columns(g0_sb, c), neg_ddg[c][:]])
            else:
                margin = reused([P, W], F32, "margin_last", "before_logs")
                nc.vector.tensor_tensor(margin[:], neg_ddg[c][:], columns(g0_sb, c), ALU.add)
            tanh_sb[c] = keep.tile([P, W], F32, name=f"tanh{c}")
            nc.scalar.activation(out=tanh_sb[c][:], in_=margin[:], func=ACT.Tanh, scale=0.5)

        def capped(c, dst):
            acr[c] = dst
            nc.vector.tensor_tensor(dst, boltz[c][:], columns(cap_sb, c), ALU.min)

        products(0)
        for step in range(len(CHUNKS) + LAG):
            if step <= LAST:
                gather_first(step)
            if step == 2 * LAG:
                capped(0, reused([P, W], F32, "acr0", f"chunk{step - 1}")[:])
            if 1 <= step <= LAST + 1:
                close(step - 1)
            if step <= LAST:
                gather_second(step)
                if step % HALVES == 0 and step // HALVES + 1 < PACK:
                    products(step // HALVES + 1)
            if step >= LAG:
                done = step - LAG
                functions(done)
                if done % HALVES == 1 and done // HALVES + 2 < PACK:
                    load_g0(done // HALVES + 2)
                    load_cap(done // HALVES + 2)

        by_halves = [t * HALVES + h for h in range(HALVES) for t in range(PACK)]
        acr_late = reused([P, LAST, W], F32, "acr_late", "after_gathers")
        for n, c in enumerate(by_halves[1:]):
            capped(c, acr_late[:, n, :])

        w3_scale_sb = reused([P, 1, N], U8, "w3_scale", "load0")
        nc.gpsimd.memset(w3_scale_sb[:].bitcast(I32), 0)
        load_scales(w3_scale_sb[:], w3_scales)

        logs = reused([P, len(CHUNKS), W], F32, "logs", "before_logs")
        summed = [keep.tile([P, PACK, W], F32, name=f"summed{h}") for h in range(HALVES)]
        for c in by_halves:
            t, h = CHUNKS[c]
            nc.scalar.activation(out=logs[:, c, :], in_=acr[c], func=ACT.Ln, scale=LOG_SCALE, bias=0.2 * LOG_SCALE)
            if c != LAST:
                tanh_rows = turned_sum(psum.tile([P, W], F32, name="tanh_rows", tag=f"back{t % 2}"), [tanh_sb[c][:]])
            else:
                tanh_rows = tanh_sb[c]
            nc.vector.scalar_tensor_tensor(
                out=summed[h][:, t, :], in0=logs[:, c, :], scalar=-0.8, in1=tanh_rows[:], op0=ALU.mult, op1=ALU.add
            )

        def scaled(h):
            hid_rows = keep.tile([P, PACK, W], BF16, name=f"hid_rows{h}")
            for t in range(PACK):
                factor = half_unit[:, t : t + 1]
                if h == 0 or t < GPSIMD_TILES:
                    nc.gpsimd.tensor_scalar(
                        out=hid_rows[:, t, :], in0=summed[h][:, t, :], scalar1=factor, scalar2=0.0, op0=ALU.mult, op1=ALU.add
                    )
                else:
                    nc.scalar.activation(out=hid_rows[:, t, :], in_=summed[h][:, t, :], func=ACT.Copy, scale=factor)
            return hid_rows

        def interleaved(hid_rows, first, width):
            hid = keep.tile([P, width * PACK], BF16, name=f"hid{first}", align_bytes=64)
            nc.vector.tensor_copy(
                out=hid[:].rearrange("p (c i t) -> p c t i", i=4, t=PACK),
                in_=hid_rows[:, :, first % W : first % W + width].rearrange("p t (c i) -> p c t i", i=4),
            )
            return hid

        def last_product(hid, first, width):
            codes = keep.tile([P, width], U32, name=f"codes{first}", align_bytes=64)
            hid_scales = keep.tile([P, width], U8, name=f"hid_scales{first}", align_bytes=64)
            nc.vector.quantize_mx(out=codes[:].bitcast(FP8X4), scales=hid_scales[:], in_=hid[:])
            for m in range(N // P):
                acc = psum.tile([P, width], F32, name="out_acc", tag=("product", "margin")[m])
                nc.tensor.matmul_mx(
                    out=acc[:],
                    lhsT=w3_word_sb[:, 2 * m * P : 2 * (m + 1) * P].bitcast(FP4X4),
                    lhsT_scale=w3_scale_sb[:, 0, m * P : (m + 1) * P],
                    rhs=codes[:].bitcast(FP8X4),
                    rhs_scale=hid_scales[:],
                    start=True,
                    stop=True,
                )
                result = keep.tile([P, width], F32, name=f"result{first}_{m}")
                if first >= W and m == 1:
                    nc.vector.tensor_copy(out=result[:], in_=acc[:])
                else:
                    nc.scalar.copy(out=result[:], in_=acc[:])
                nc.sync.dma_start(out=out[m * P : (m + 1) * P, first : first + width], in_=result[:])

        quarter = W // 2
        hid_half = interleaved(scaled(0), 0, W)
        second_rows = scaled(1)
        hid_third = interleaved(second_rows, W, quarter)
        last_product(hid_half, 0, W)
        hid_fourth = interleaved(second_rows, W + quarter, quarter)
        last_product(hid_third, W, quarter)
        last_product(hid_fourth, W + quarter, quarter)
